import numpy as np
import ml_dtypes


def mxq(x, axis, fmt="e4m3"):
    dtype, down = {"e4m3": (ml_dtypes.float8_e4m3fn, 7), "e5m2": (ml_dtypes.float8_e5m2, 14)}[fmt]
    v = np.moveaxis(np.asarray(x, np.float32).astype(ml_dtypes.bfloat16).astype(np.float64), axis, -1)
    blocks = v.reshape(v.shape[:-1] + (-1, 32))
    amax = np.abs(blocks).max(-1, keepdims=True)
    byte = np.maximum(np.where(amax > 0, np.frexp(amax)[1] - 1 + 127, 0) - down, 1)
    scale = np.exp2(byte - 127.0)
    codes = (blocks / scale).astype(np.float32).astype(dtype).astype(np.float64)
    return np.moveaxis((codes * scale).reshape(v.shape), -1, axis)


WIDE = False


def mx_kscale(k):
    if not WIDE:
        return np.ones(k)
    levels = np.array([10, -10, 5, -5, 0])
    if k % 512:
        return np.exp2(np.random.permutation(np.resize(levels, k // 32))).repeat(32)
    a = np.empty((k // 512, 16))
    for p in range(k // 512):
        a[p, :8] = np.random.permutation(np.resize(levels, 8))
        for g in range(8):
            far = levels[np.abs(levels - a[p, g]) >= 10]
            a[p, g + 8] = far[np.random.randint(len(far))]
    return np.exp2(a.ravel()).repeat(32)


BF16 = ml_dtypes.bfloat16


def bf(x):
    return np.asarray(x, np.float32).astype(BF16)


def f64(x):
    return np.asarray(x).astype(np.float64)


E2M1 = np.array([0.0, 0.5, 1.0, 1.5, 2.0, 3.0, 4.0, 6.0, -0.0, -0.5, -1.0, -1.5, -2.0, -3.0, -4.0, -6.0])


def pack_weight(w, fmt):
    k, n = w.shape
    w = f64(bf(w)).reshape(k // 32, 32, n)
    amax = np.abs(w).max(1)
    if fmt == "e4m3":
        byte = np.frexp(amax)[1] - 1 + 127 - 7
    else:
        mant, ex = np.frexp(amax / 6.0)
        byte = np.where(mant > 0.5, ex, ex - 1) + 127
    byte = np.clip(np.where(amax > 0, byte, 1), 1, 254)
    scaled = (w * np.exp2(127.0 - byte)[:, None, :]).reshape(k, n).astype(np.float32)
    by_word = np.ascontiguousarray(scaled.reshape(k // 512, 128, 4, n).transpose(0, 1, 3, 2))
    if fmt == "e4m3":
        words = by_word.astype(ml_dtypes.float8_e4m3fn).view(np.uint8)
    else:
        c = by_word.astype(ml_dtypes.float4_e2m1fn).view(np.uint8) & 0xF
        words = c[..., 0::2] | (c[..., 1::2] << 4)
    return np.ascontiguousarray(words), np.ascontiguousarray(byte.astype(np.uint8).reshape(k // 512, 16, n))


def unpack_weight(words, scales, fmt):
    g, p, n, _ = words.shape
    if fmt == "e4m3":
        vals = np.ascontiguousarray(words).view(ml_dtypes.float8_e4m3fn).astype(np.float64)
    else:
        nib = np.empty((g, p, n, 4), np.uint8)
        nib[..., 0::2] = words & 0xF
        nib[..., 1::2] = words >> 4
        vals = E2M1[nib]
    vals = vals * np.repeat(np.exp2(scales.astype(np.float64) - 127.0), 8, axis=1)[..., None]
    return vals.transpose(0, 1, 3, 2).reshape(g * 512, n)
def pack4(w):
    words, scales = pack_weight(w, "e2m1")
    return words.reshape(words.shape[0], 128, -1), scales


def unpack4(words, scales):
    return unpack_weight(words.reshape(words.shape[0], 128, -1, 2), scales, "e2m1")


T, K, O, F, N = 1536, 1024, 512, 1024, 1024
OUTLIER = 6.0


def draw0():
    s, o = mx_kscale(K), mx_kscale(O)
    t = mx_kscale(T)
    x = np.random.standard_normal((T, K)) * s
    xo = OUTLIER * np.random.standard_normal((T, O)) * o
    w = np.random.standard_normal((K, F)) / np.sqrt(K) / s[:, None]
    wo = np.random.standard_normal((O, F)) / np.sqrt(O) / OUTLIER / o[:, None]
    gate = np.random.uniform(0.25, 1.0, T) * t
    dy = 2.0 * np.random.standard_normal((T, N)) / np.sqrt(T) / t[:, None]
    w_words, w_scales = pack4(w)
    dy_words, dy_scales = pack4(dy)
    return {"x": bf(x), "xo": bf(xo), "w_words": w_words, "w_scales": w_scales,
            "wo": bf(wo), "gate": bf(gate), "dy_words": dy_words, "dy_scales": dy_scales}


def core(x, xo, w_words, w_scales, wo, gate, dy_words, dy_scales):
    base = mxq(f64(x), 1, "e4m3") @ unpack4(w_words, w_scales)
    outl = mxq(f64(xo), 1, "e4m3") @ mxq(f64(wo), 0, "e4m3")
    h = np.maximum(base + outl, 0.0) * f64(gate)[:, None]
    dw = mxq(h, 0, "e4m3").T @ unpack4(dy_words, dy_scales)
    return dw


def e4m3fn_bytes(y):
    return np.clip(np.asarray(y, np.float64), -448.0, 448.0).astype(np.float32).astype(ml_dtypes.float8_e4m3fn).view(np.uint8)


def e4m3fn_values(b):
    return np.asarray(b, np.uint8).view(ml_dtypes.float8_e4m3fn).astype(np.float64)


def setup_inputs():
    d = draw0()
    x0 = np.asarray(d['x']).astype(np.float64)
    s = (np.max(np.abs(x0), axis=(0,), keepdims=True) / 448.0).astype(np.float32)
    out = {}
    for k, v in d.items():
        if k == 'x':
            out['x_bytes'] = e4m3fn_bytes(x0 / s.astype(np.float64))
            out['x_scale'] = s
        else:
            out[k] = v
    return out


def reference(x_bytes, x_scale, xo, w_words, w_scales, wo, gate, dy_words, dy_scales):
    return core(e4m3fn_values(x_bytes) * x_scale.astype(np.float64), xo, w_words, w_scales, wo, gate, dy_words, dy_scales)

from contextlib import ExitStack

import concourse.mybir as mybir
from concourse.masks import make_identity

T, K, O, F, N = 1536, 1024, 512, 1024, 1024
FLOPS = 2 * T * F * (K + O) + 2 * T * F * N

F32 = mybir.dt.float32
BF16 = mybir.dt.bfloat16
U32 = mybir.dt.uint32
U8 = mybir.dt.uint8
I32 = mybir.dt.int32
FP8 = mybir.dt.float8_e4m3fn
FP8X4 = mybir.dt.float8_e4m3fn_x4
FP4X4 = mybir.dt.float4_e2m1fn_x4
MULT = mybir.AluOpType.mult
MAX = mybir.AluOpType.max

P = 128
G = T // 512
PAIRS = 2 * G
CH = F // P


def tile_recomputed_hidden_weight_gradient_s3_kernel(
    tc, x_bytes, x_scale, xo, w_words, w_scales, wo, gate, dy_words, dy_scales, out
):
    nc = tc.nc
    with ExitStack() as ctx:
        keep = ctx.enter_context(tc.tile_pool(name="keep", bufs=1))
        hpool = ctx.enter_context(tc.tile_pool(name="hpool", bufs=4))
        psum_a = ctx.enter_context(tc.psum_pool(name="psum_a", bufs=4))
        psum_h = ctx.enter_context(tc.psum_pool(name="psum_h", bufs=4))
        ctx.enter_context(tc.manual_schedule())

        ident = keep.tile([P, P], F32, name="ident", align_bytes=64)
        wt = keep.tile([P, 2, 2 * F], U8, name="wt", align_bytes=64)
        ws = keep.tile([P, 2, F], U8, name="ws", align_bytes=64)
        dyt = keep.tile([P, G, 2 * N], U8, name="dyt", align_bytes=64)
        dys = keep.tile([P, G, N], U8, name="dys", align_bytes=64)
        sc = keep.tile([P, 2, 4], F32, name="sc", align_bytes=64)
        gt = keep.tile([P, G, 4], BF16, name="gt", align_bytes=64)
        woq = keep.tile([P, F], U32, name="woq", align_bytes=64)
        wos = keep.tile([P, F], U8, name="wos", align_bytes=64)

        xbytes, xb, xor, xg, xog, xq, xs = [], [], [], [], [], [], []
        for pr in range(PAIRS):
            xbytes.append(keep.tile([P, 2, K], U8, name="xbytes%d" % pr, align_bytes=64))
            xb.append(keep.tile([P, 2 * K], BF16, name="xb%d" % pr, align_bytes=64))
            xor.append(keep.tile([P, 2 * O], BF16, name="xor%d" % pr, align_bytes=64))
            xg.append(keep.tile([P, 2, 1024], BF16, name="xg%d" % pr, align_bytes=64))
            xog.append(keep.tile([P, 1024], BF16, name="xog%d" % pr, align_bytes=64))
            xq.append(keep.tile([P, 3, 256], U32, name="xq%d" % pr, align_bytes=64))
            xs.append(keep.tile([P, 3, 256], U8, name="xs%d" % pr, align_bytes=64))
        wor, wog = [], []
        for hf in range(2):
            wor.append(keep.tile([P, 4, 512], BF16, name="wor%d" % hf, align_bytes=64))
            wog.append(keep.tile([P, 2048], BF16, name="wog%d" % hf, align_bytes=64))
        hq, hs = [], []
        for g in range(G):
            hq.append(keep.tile([P, F], U32, name="hq%d" % g, align_bytes=64))
            hs.append(keep.tile([P, F], U8, name="hs%d" % g, align_bytes=64))
        ot = []
        for m in range(CH):
            ot.append(keep.tile([P, N], F32, name="ot%d" % m, align_bytes=64))

        nc.vector.memset(ws[:].rearrange("p g n -> p (g n)").bitcast(I32), 0)
        nc.vector.memset(dys[:].rearrange("p g n -> p (g n)").bitcast(I32), 0)
        make_identity(nc, ident[:])

        x_v = x_bytes.rearrange("(g m t) k -> g m t k", m=P, t=4)
        xo_v = xo.rearrange("(g m t) k -> g m t k", m=P, t=4)
        wo_v = wo.rearrange("(p j) f -> p j f", j=4)

        def load_x(pr):
            g, h = divmod(pr, 2)
            nc.sync.dma_start(out=xbytes[pr][:], in_=x_v[g][:, 2 * h : 2 * h + 2, :])

        def load_xo(pr):
            g, h = divmod(pr, 2)
            nc.sync.dma_start(
                out=xor[pr][:].rearrange("p (t k) -> p t k", t=2),
                in_=xo_v[g][:, 2 * h : 2 * h + 2, :],
            )

        def load_wo(hf):
            nc.sync.dma_start(out=wor[hf][:], in_=wo_v[:, :, 512 * hf : 512 * hf + 512])

        def load_scales(dst, src):
            for q in range(4):
                nc.sync.dma_start(
                    out=dst[32 * q : 32 * q + 4, :, :].bitcast(I32),
                    in_=src.rearrange("g q n -> q g n")[4 * q : 4 * q + 4, :, :].bitcast(I32),
                )

        load_x(0)
        load_xo(0)
        nc.sync.dma_start(
            out=sc[:], in_=x_scale.rearrange("o (g p t) -> p (o g) t", p=P, t=4)
        )
        load_wo(0)
        load_x(1)
        load_xo(1)
        load_scales(ws, w_scales)
        nc.sync.dma_start(out=wt[:], in_=w_words.rearrange("g p n -> p g n"))
        nc.sync.dma_start(out=gt[:], in_=gate.rearrange("(g m t) -> m g t", m=P, t=4))
        load_x(2)
        load_xo(2)
        load_wo(1)
        for pr in range(3, PAIRS):
            load_x(pr)
            load_xo(pr)
        load_scales(dys, dy_scales)
        nc.sync.dma_start(out=dyt[:], in_=dy_words.rearrange("g p n -> p g n"))

        def cast_s(pr, t):
            nc.scalar.copy(
                out=xb[pr][:, K * t : K * t + K], in_=xbytes[pr][:, t, :].bitcast(FP8)
            )

        def cast_v(pr, t):
            nc.vector.tensor_copy(
                out=xb[pr][:, K * t : K * t + K], in_=xbytes[pr][:, t, :].bitcast(FP8)
            )

        xps = {}

        def turn(pr):
            po = psum_a.tile([P, 512], F32, name="a")
            words = xor[pr][:].bitcast(F32)
            for t in range(2):
                for u in range(2):
                    c0 = 256 * t + u
                    nc.tensor.transpose(
                        po[:, 256 * u + P * t : 256 * u + P * t + P],
                        words[:, c0 : 256 * t + 256 : 2],
                        ident[:],
                    )
            px = [psum_a.tile([P, 512], F32, name="a"), psum_a.tile([P, 512], F32, name="a")]
            words = xb[pr][:].bitcast(F32)
            for g in range(2):
                for t in range(2):
                    for u in range(2):
                        c0 = 512 * t + 256 * g
                        nc.tensor.transpose(
                            px[g][:, 256 * u + P * t : 256 * u + P * t + P],
                            words[:, c0 + u : c0 + 256 : 2],
                            ident[:],
                        )
            xps[pr] = (px[0], px[1], po)

        def xo_out(pr):
            nc.scalar.copy(
                out=xog[pr][:].bitcast(F32).rearrange("p (r u) -> p r u", u=2),
                in_=xps[pr][2][:].rearrange("p (u r) -> p r u", u=2),
            )

        def prod(pr, g):
            nc.vector.tensor_tensor(
                out=xg[pr][:, g, :].rearrange("p (r u e) -> p r u e", u=2, e=2),
                in0=xps[pr][g][:].bitcast(BF16).rearrange("p (u r e) -> p r u e", u=2, e=2),
                in1=sc[:, g, :]
                .rearrange("p (u e) -> p u e", e=2)
                .unsqueeze(1)
                .to_broadcast([P, 256, 2, 2]),
                op=MULT,
            )

        def quant_x(pr, g):
            nc.vector.quantize_mx(
                out=xq[pr][:, g, :].bitcast(FP8X4), scales=xs[pr][:, g, :], in_=xg[pr][:, g, :]
            )

        def quant_xo(pr):
            nc.vector.quantize_mx(
                out=xq[pr][:, 2, :].bitcast(FP8X4), scales=xs[pr][:, 2, :], in_=xog[pr][:]
            )

        def wo_lay(engine_copy, hf):
            engine_copy(
                out=wog[hf][:].rearrange("p (c i t) -> p c t i", i=4, t=4),
                in_=wor[hf][:].rearrange("p t (c i) -> p c t i", i=4),
            )

        def quant_wo(hf):
            cols = slice(512 * hf, 512 * hf + 512)
            nc.vector.quantize_mx(
                out=woq[:, cols].bitcast(FP8X4), scales=wos[:, cols], in_=wog[hf][:]
            )

        hps = {}

        def stage1(g, c, ts):
            if 0 in ts:
                hps[g, c] = psum_h.tile([P, 512], F32, name="h")
            acc = hps[g, c]
            f0 = P * c
            for t in ts:
                pr, tl = 2 * g + t // 2, t % 2
                r = slice(P * tl, P * tl + P)
                for kk in range(3):
                    if kk < 2:
                        rhs = wt[:, kk, 2 * f0 : 2 * f0 + 2 * P].bitcast(FP4X4)
                        rsc = ws[:, kk, f0 : f0 + P]
                    else:
                        rhs = woq[:, f0 : f0 + P].bitcast(FP8X4)
                        rsc = wos[:, f0 : f0 + P]
                    nc.tensor.matmul_mx(
                        out=acc[:, P * t : P * t + P],
                        lhsT=xq[pr][:, kk, r].bitcast(FP8X4),
                        lhsT_scale=xs[pr][:, kk, r],
                        rhs=rhs,
                        rhs_scale=rsc,
                        start=(kk == 0),
                        stop=(kk == 2),
                    )

        hgt = {}

        def hid(g, c):
            hgt[g, c] = hpool.tile([P, 512], BF16, name="hg", align_bytes=64)
            nc.vector.scalar_tensor_tensor(
                out=hgt[g, c][:].rearrange("p (f t) -> p f t", t=4),
                in0=hps[g, c][:].rearrange("p (t f) -> p f t", t=4),
                scalar=0.0,
                in1=gt[:, g, :].unsqueeze(1).to_broadcast([P, P, 4]),
                op0=MAX,
                op1=MULT,
            )

        def quant_h(g, c):
            cols = slice(P * c, P * c + P)
            nc.vector.quantize_mx(
                out=hq[g][:, cols].bitcast(FP8X4), scales=hs[g][:, cols], in_=hgt[g, c][:]
            )

        dwp = {}

        def stage2(m):
            cols = slice(P * m, P * m + P)
            for nh in range(2):
                acc = psum_a.tile([P, 512], F32, name="a")
                for g in range(G):
                    nc.tensor.matmul_mx(
                        out=acc[:],
                        lhsT=hq[g][:, cols].bitcast(FP8X4),
                        lhsT_scale=hs[g][:, cols],
                        rhs=dyt[:, g, 1024 * nh : 1024 * nh + 1024].bitcast(FP4X4),
                        rhs_scale=dys[:, g, 512 * nh : 512 * nh + 512],
                        start=(g == 0),
                        stop=(g == G - 1),
                    )
                dwp[m, nh] = acc

        def store(m):
            nc.scalar.copy(out=ot[m][:, 0:512], in_=dwp[m, 0][:])
            nc.vector.tensor_copy(out=ot[m][:, 512:1024], in_=dwp[m, 1][:])
            for nh in range(2):
                nc.sync.dma_start(
                    out=out[P * m : P * m + P, 512 * nh : 512 * nh + 512],
                    in_=ot[m][:, 512 * nh : 512 * nh + 512],
                )

        cast_v(0, 0)
        cast_s(0, 1)
        turn(0)
        wo_lay(nc.vector.tensor_copy, 0)
        cast_v(1, 0)
        cast_s(1, 1)
        xo_out(0)
        prod(0, 0)
        quant_wo(0)
        prod(0, 1)
        quant_x(0, 0)
        quant_xo(0)
        quant_x(0, 1)
        turn(1)
        for c in range(4):
            stage1(0, c, (0, 1))
        xo_out(1)
        cast_s(2, 0)
        cast_s(2, 1)
        prod(1, 0)
        prod(1, 1)
        quant_x(1, 0)
        quant_xo(1)
        quant_x(1, 1)
        wo_lay(nc.scalar.copy, 1)
        turn(2)
        xo_out(2)

        def block(g, c0, pr, ts):
            if pr + 1 < PAIRS:
                cast_s(pr + 1, 0)
                cast_s(pr + 1, 1)
            prod(pr, 0)
            stage1(g, c0, ts)
            hid(g, c0)
            prod(pr, 1)
            quant_x(pr, 0)
            quant_h(g, c0)
            stage1(g, c0 + 1, ts)
            hid(g, c0 + 1)
            quant_xo(pr)
            quant_x(pr, 1)
            quant_h(g, c0 + 1)
            stage1(g, c0 + 2, ts)
            stage1(g, c0 + 3, ts)
            hid(g, c0 + 2)
            if g == 0 and c0 == 0:
                quant_wo(1)
            hid(g, c0 + 3)
            quant_h(g, c0 + 2)
            quant_h(g, c0 + 3)
            if pr + 1 < PAIRS:
                turn(pr + 1)
                xo_out(pr + 1)

        allt = (0, 1, 2, 3)
        block(0, 0, 2, (2, 3))
        block(0, 4, 3, allt)
        block(1, 0, 4, allt)
        block(1, 4, 5, allt)
        for c in range(CH + 2):
            if c < CH:
                stage1(2, c, allt)
                hid(2, c)
            if c >= 2:
                stage2(c - 2)
            if c < CH:
                quant_h(2, c)
            if c >= 2:
                store(c - 2)
